import numpy as np
CORES = [30,6,62,38,9,49,17,41]
N = 8
def setup_inputs(rng):
    return {"x": rng.standard_normal((N, 128, 256), dtype=np.float32)}
def reference(x):
    s = x.sum(axis=0, dtype=np.float64).astype(x.dtype)
    return {"y": np.broadcast_to(s, (N,) + s.shape)}

from concourse.mybir import AluOpType

RING_CHIPS = [4, 2, 6, 0, 3, 1, 5, 7]
NB = 8
ROWS = 16
SCRATCH = {
    "buf": ("dram", [2, 128, 32], "float32"),
}
SEMAPHORES = ["land", "cred", "acc", "d"]


def rank_program(g, core, T, topo):
    if T.rank_of(core) is None:
        return
    by_chip = {}
    for c in T.cores:
        by_chip[topo.chip(c)] = c
    ring = [by_chip[ch] for ch in RING_CHIPS]
    p = ring.index(core)
    succ = ring[(p + 1) % NB]
    pred = ring[(p - 1) % NB]
    s_rid, s_pid, _ = topo.addr(succ)
    p_rid, p_pid, _ = topo.addr(pred)
    land, cred, acc, d = T.sem.land, T.sem.cred, T.sem.acc, T.sem.d

    def xb(s):
        b = (p - s) % NB
        return T.x[b * ROWS:(b + 1) * ROWS, :]

    def yb(s):
        b = (p - s) % NB
        return T.y[b * ROWS:(b + 1) * ROWS, :]

    n = {"land": 0, "d": 0, "acc": 0}

    def send(s):
        g.remote_dma(T.buf[(s + 1) % 2], T.buf[s % 2], land, land, s_pid, s_rid, 0xFF)
        n["land"] += 8

    def credit():
        g.remote_sem_update(cred, land, p_pid, p_rid, 0x1)
        n["land"] += 1

    def go_drain(s):
        g.sem_inc(d, 1)
        n["d"] += 1
        g.sync.wait_ge(d, n["d"])
        g.sync.dma_start(yb(s), T.buf[s % 2]).then_inc(d, 16)
        n["d"] += 16

    g.sync.dma_start(T.buf[0], xb(0)).then_inc(d, 16)
    n["d"] += 16
    g.wait_ge(d, n["d"])
    send(0)

    for s in range(1, 14):
        n["land"] += 8
        g.wait_ge(land, n["land"])
        if s <= 7:
            g.dma_start(T.buf[s % 2], xb(s), accum_op=AluOpType.add, max_dma_last_dim=8192).then_inc(acc, 16)
            n["acc"] += 16
            credit()
            g.wait_ge(acc, n["acc"])
            if s == 7:
                go_drain(s)
        else:
            g.wait_ge(d, n["d"])
            go_drain(s)
            credit()
        g.wait_ge(cred, s)
        send(s)

    n["land"] += 8
    g.wait_ge(land, n["land"])
    g.wait_ge(d, n["d"])
    go_drain(14)
    g.wait_ge(d, n["d"])
